import numpy as np
import ml_dtypes


def mxq(x, axis, fmt="e4m3"):
    dtype, down = {"e4m3": (ml_dtypes.float8_e4m3fn, 7), "e5m2": (ml_dtypes.float8_e5m2, 14)}[fmt]
    v = np.moveaxis(np.asarray(x, np.float32).astype(ml_dtypes.bfloat16).astype(np.float64), axis, -1)
    blocks = v.reshape(v.shape[:-1] + (-1, 32))
    amax = np.abs(blocks).max(-1, keepdims=True)
    byte = np.maximum(np.where(amax > 0, np.frexp(amax)[1] - 1 + 127, 0) - down, 1)
    scale = np.exp2(byte - 127.0)
    codes = (blocks / scale).astype(np.float32).astype(dtype).astype(np.float64)
    return np.moveaxis((codes * scale).reshape(v.shape), -1, axis)


WIDE = False


def mx_kscale(k):
    if not WIDE:
        return np.ones(k)
    levels = np.array([10, -10, 5, -5, 0])
    if k % 512:
        return np.exp2(np.random.permutation(np.resize(levels, k // 32))).repeat(32)
    a = np.empty((k // 512, 16))
    for p in range(k // 512):
        a[p, :8] = np.random.permutation(np.resize(levels, 8))
        for g in range(8):
            far = levels[np.abs(levels - a[p, g]) >= 10]
            a[p, g + 8] = far[np.random.randint(len(far))]
    return np.exp2(a.ravel()).repeat(32)


def f64(x):
    return np.asarray(x).astype(np.float64)


def striped(idx):
    return np.tile(idx.reshape(-1, 16).T, (8, 1)).astype(np.uint16)


def unstriped(offs):
    return offs[:16].T.reshape(-1).astype(np.int64)


E2M1 = np.array([0.0, 0.5, 1.0, 1.5, 2.0, 3.0, 4.0, 6.0, -0.0, -0.5, -1.0, -1.5, -2.0, -3.0, -4.0, -6.0])


def pack_weight(w, fmt):
    k, n = w.shape
    w = f64(np.asarray(w, np.float32).astype(ml_dtypes.bfloat16)).reshape(k // 32, 32, n)
    amax = np.abs(w).max(1)
    if fmt == "e4m3":
        byte = np.frexp(amax)[1] - 1 + 127 - 7
    else:
        mant, ex = np.frexp(amax / 6.0)
        byte = np.where(mant > 0.5, ex, ex - 1) + 127
    byte = np.clip(np.where(amax > 0, byte, 1), 1, 254)
    scaled = (w * np.exp2(127.0 - byte)[:, None, :]).reshape(k, n).astype(np.float32)
    by_word = np.ascontiguousarray(scaled.reshape(k // 512, 128, 4, n).transpose(0, 1, 3, 2))
    if fmt == "e4m3":
        words = by_word.astype(ml_dtypes.float8_e4m3fn).view(np.uint8)
    else:
        c = by_word.astype(ml_dtypes.float4_e2m1fn).view(np.uint8) & 0xF
        words = (c[..., 0::2] | (c[..., 1::2] << 4)).reshape(k // 512, 128, 2 * n)
    return np.ascontiguousarray(words), np.ascontiguousarray(byte.astype(np.uint8).reshape(k // 512, 16, n))


def unpack_weight(words, scales, fmt):
    g, _, n = scales.shape
    words = np.ascontiguousarray(words).reshape(g, 128, n, -1)
    if fmt == "e4m3":
        vals = words.view(ml_dtypes.float8_e4m3fn).astype(np.float64)
    else:
        nib = np.empty((g, 128, n, 4), np.uint8)
        nib[..., 0::2] = words & 0xF
        nib[..., 1::2] = words >> 4
        vals = E2M1[nib]
    vals = vals * np.repeat(np.exp2(scales.astype(np.float64) - 127.0), 8, axis=1)[..., None]
    return vals.transpose(0, 1, 3, 2).reshape(g * 512, n)


def gelu(v):
    return 0.5 * v * (1.0 + np.tanh(np.sqrt(2.0 / np.pi) * (v + 0.044715 * v**3)))


K, H, N, T, S, P, T2 = 1024, 1024, 384, 4096, 1024, 1024, 2048


def setup_inputs():
    n = np.random.standard_normal
    s = mx_kscale(K)[:, None]
    u = mx_kscale(H)[:, None]
    d = {}
    d["tab_words"], d["tab_scales"] = pack_weight(n((K, T)) * s, "e4m3")
    d["offs"] = striped(np.random.permutation(T)[:S])
    d["offs2"] = striped(np.random.permutation(T2)[:S])
    d["offs3"] = striped(np.random.permutation(T2)[:P])
    d["offs4"] = striped(np.random.permutation(T2)[:P])
    d["w1"] = (n((K, H)) / K**0.5 / s).astype(np.float32)
    d["w2_words"], d["w2_scales"] = pack_weight(n((K, H)) / K**0.5 / s, "e2m1")
    d["gain"] = (0.6 * np.exp(0.3 * n(H)) * u[:, 0]).astype(np.float32)
    d["wgs"] = np.exp(0.3 * n((128, S))).astype(np.float32)
    d["page0"] = (n((H, T2)) * u).astype(np.float32)
    d["roast"] = (0.7 * n((H, P)) * u).astype(np.float32)
    d["w3_words"], d["w3_scales"] = pack_weight(n((H, N)) / H**0.5 / u, "e4m3")
    d["wgo"] = np.exp(0.3 * n((128, P))).astype(np.float32)
    d["page1"] = n((N, T2)).astype(np.float32)
    return d


def reference(tab_words, tab_scales, offs, offs2, offs3, offs4, w1, w2_words, w2_scales,
              gain, wgs, page0, roast, w3_words, w3_scales, wgo, page1):
    v = unpack_weight(tab_words, tab_scales, "e4m3")[:, unstriped(offs)]
    a = mxq(f64(w1), 0, "e4m3").T @ v
    b = unpack_weight(w2_words, w2_scales, "e2m1").T @ v
    h = f64(gain)[:, None] * (a * b + a + b)
    page = f64(page0).copy()
    page[:, unstriped(offs2)] = np.tile(f64(wgs), (H // 128, 1)) * h
    x = page[:, unstriped(offs3)] + f64(roast)
    y = np.abs(unpack_weight(w3_words, w3_scales, "e4m3").T @ mxq(x, 0, "e4m3"))
    out = f64(page1).copy()
    out[:, unstriped(offs4)] = np.tile(f64(wgo), (N // 128, 1)) * y
    return out

@@ -1,0 +1,315 @@
+from contextlib import ExitStack
+
+import concourse.mybir as mybir
+from concourse.masks import make_identity
+
+K, H, N, T, S, PICKS, T2 = 1024, 1024, 384, 4096, 1024, 1024, 2048
+FLOPS = 2 * (2 * K * H * S + H * N * PICKS)
+
+F32 = mybir.dt.float32
+BF16 = mybir.dt.bfloat16
+I32 = mybir.dt.int32
+U32 = mybir.dt.uint32
+U16 = mybir.dt.uint16
+U8 = mybir.dt.uint8
+FP8X4 = mybir.dt.float8_e4m3fn_x4
+FP4X4 = mybir.dt.float4_e2m1fn_x4
+ADD = mybir.AluOpType.add
+MULT = mybir.AluOpType.mult
+ACT = mybir.ActivationFunctionType
+
+P = 128
+PASSES = 2
+HALF = 512
+LIST_COLS = HALF // 16
+ROW_TILES = H // P
+OUT_TILES = N // P
+W1_COLS = 256
+SUB = HALF // P
+
+
+def tile_list_bean_lot_recall_kernel(
+    tc, tab_words, tab_scales, offs, offs2, offs3, offs4, w1, w2_words, w2_scales,
+    gain, wgs, page0, roast, w3_words, w3_scales, wgo, page1, out,
+):
+    nc = tc.nc
+    with ExitStack() as ctx:
+        keep = ctx.enter_context(tc.tile_pool(name="keep", bufs=1))
+        ring = ctx.enter_context(tc.tile_pool(name="ring", bufs=2))
+        psum = ctx.enter_context(tc.psum_pool(name="psum", bufs=1))
+        a_bank = [psum.tile([P, HALF], F32, name=f"a_bank{i}") for i in range(2)]
+        b_bank = [psum.tile([P, HALF], F32, name=f"b_bank{i}") for i in range(2)]
+        x_bank = [psum.tile([P, HALF], F32, name=f"x_bank{i}") for i in range(2)]
+        w_bank = [psum.tile([P, HALF], F32, name=f"w_bank{i}") for i in range(2)]
+
+        def load_list(src, name):
+            tile = keep.tile([P, S // 16], U16, name=name)
+            nc.sync.dma_start(tile[:], src)
+            return tile
+
+        def load_scales(src, tile, queue):
+            nc.vector.memset(tile[:].bitcast(I32), 0)
+            for q in range(4):
+                queue.dma_start(
+                    out=tile[32 * q : 32 * q + 4, :].bitcast(I32).rearrange("r (a c) -> r a c", a=PASSES),
+                    in_=src[:, 4 * q : 4 * q + 4, :].bitcast(I32).rearrange("a r c -> r a c"),
+                )
+
+        def load_table_words(a):
+            tile = ring.tile([P, T], I32, name=f"tabw{a}", tag="tabw")
+            nc.sync.dma_start(out=tile[:], in_=tab_words[a].rearrange("p t i -> p (t i)").bitcast(I32))
+            return tile
+
+        w1_raw = {}
+
+        def load_w1(c):
+            for a in range(PASSES):
+                tile = ring.tile([P, 4, W1_COLS], F32, name=f"w1raw{c}_{a}", tag="stage", bufs=4)
+                rows = w1[HALF * a : HALF * (a + 1), W1_COLS * c : W1_COLS * (c + 1)]
+                nc.sync.dma_start(out=tile[:], in_=rows.rearrange("(p j) c -> p j c", j=4))
+                w1_raw[c, a] = tile
+
+        pages, roasts = {}, {}
+
+        def load_page(t):
+            pages[t] = keep.tile([P, T2], F32, name=f"page{t}")
+            nc.sync.dma_start(out=pages[t][:], in_=page0[P * t : P * (t + 1), :])
+
+        def load_roast_first(t):
+            tile = keep.tile([P, HALF], F32, name=f"roast{t}")
+            nc.sync.dma_start(out=tile[:], in_=roast[P * t : P * (t + 1), 0:HALF])
+            roasts[t, 0] = tile[:]
+
+        def load_roast_second(t):
+            tile = ring.tile([P, 2, HALF], F32, name=f"roastb{t}", tag="stage", bufs=4)
+            rows = roast[P * t : P * (t + 2), HALF:PICKS]
+            nc.sync.dma_start(out=tile[:], in_=rows.rearrange("(u p) m -> p u m", u=2))
+            roasts[t, 1] = tile[:, 0, :]
+            roasts[t + 1, 1] = tile[:, 1, :]
+
+        list1 = load_list(offs, "list1")
+        list2 = load_list(offs2, "list2")
+        list3 = load_list(offs3, "list3")
+        list4 = load_list(offs4, "list4")
+        tab_s = keep.tile([P, PASSES * T], U8, name="tab_s", tag="tabs")
+        load_scales(tab_scales, tab_s, nc.scalar)
+        w2_s = keep.tile([P, PASSES * H], U8, name="w2_s", align_bytes=64)
+        load_scales(w2_scales, w2_s, nc.scalar)
+        gain_rows = keep.tile([P, P], F32, name="gain_rows")
+        nc.vector.memset(gain_rows[:], 0.0)
+        nc.gpsimd.dma_start(out=gain_rows[0:ROW_TILES, :], in_=gain.rearrange("(t p) -> t p", p=P))
+        ident = keep.tile([P, P], F32, name="ident")
+        make_identity(nc, ident[:])
+        w3_s = keep.tile([P, PASSES * N], U8, name="w3_s", align_bytes=64)
+        load_scales(w3_scales, w3_s, nc.gpsimd)
+
+        tab_w = [load_table_words(0)]
+        load_w1(0)
+        w2_w = keep.tile([P, PASSES * 2 * H], U8, name="w2_w", align_bytes=64)
+        nc.sync.dma_start(
+            out=w2_w[:].bitcast(I32).rearrange("p (a c) -> p a c", a=PASSES),
+            in_=w2_words.bitcast(I32).rearrange("a p c -> p a c"),
+        )
+        tab_w.append(load_table_words(1))
+        load_w1(1)
+        wgs_t = keep.tile([P, S], F32, name="wgs_t")
+        nc.sync.dma_start(out=wgs_t[:], in_=wgs)
+        load_page(0)
+        for t in range(ROW_TILES):
+            if t + 1 < ROW_TILES:
+                load_page(t + 1)
+            if t + 2 < H // W1_COLS:
+                load_w1(t + 2)
+            load_roast_first(t)
+        w3_w = keep.tile([P, PASSES * N], U32, name="w3_w", align_bytes=64)
+        nc.sync.dma_start(
+            out=w3_w[:].bitcast(I32).rearrange("p (a c) -> p a c", a=PASSES),
+            in_=w3_words.rearrange("a p c i -> a p (c i)").bitcast(I32).rearrange("a p c -> p a c"),
+        )
+        wgo_t = keep.tile([P, PICKS], F32, name="wgo_t")
+        nc.sync.dma_start(out=wgo_t[:], in_=wgo)
+
+        v_s, v_w = [], {}
+        for a in range(PASSES):
+            tile = keep.tile([P, S], U8, name=f"v_s{a}", align_bytes=64)
+            nc.vector.tensor_copy(tile[:], tab_s[:, T * a : T * (a + 1)].indirect(list1[:]))
+            v_s.append(tile)
+        for a in range(PASSES):
+            for jh in range(2):
+                tile = keep.tile([P, HALF], U32, name=f"v_w{a}_{jh}", align_bytes=64)
+                picks = list1[:, LIST_COLS * jh : LIST_COLS * (jh + 1)]
+                nc.vector.tensor_copy(tile[:], tab_w[a][:].bitcast(U32).indirect(picks))
+                v_w[a, jh] = tile
+
+        gain_ps = x_bank[0]
+        nc.tensor.transpose(gain_ps[:, 0:P], gain_rows[:], ident[:])
+        gain_t = keep.tile([P, ROW_TILES], F32, name="gain_t")
+        nc.scalar.copy(gain_t[:], gain_ps[:, 0:ROW_TILES])
+
+        w1_w, w1_s = {}, {}
+
+        def quantise_w1(c):
+            grouped = ring.tile([P, PASSES * W1_COLS * 4], BF16, name=f"w1g{c}", tag="grouped", align_bytes=64)
+            for a in range(PASSES):
+                dst = grouped[:, 4 * W1_COLS * a : 4 * W1_COLS * (a + 1)]
+                nc.scalar.copy(
+                    dst.rearrange("p (c i j) -> p c j i", i=4, j=4),
+                    w1_raw[c, a][:].rearrange("p j (c i) -> p c j i", i=4),
+                )
+            w1_w[c] = keep.tile([P, PASSES * W1_COLS], U32, name=f"w1w{c}", align_bytes=64)
+            w1_s[c] = keep.tile([P, PASSES * W1_COLS], U8, name=f"w1s{c}", align_bytes=64)
+            nc.vector.quantize_mx(out=w1_w[c][:].bitcast(FP8X4), scales=w1_s[c][:], in_=grouped[:])
+
+        h_buf = [keep.tile([P, S], F32, name=f"h_buf{i}") for i in range(2)]
+        b_buf = [[keep.tile([P, HALF], F32, name=f"b_buf{jh}_{i}") for i in range(3 - jh)] for jh in range(2)]
+
+        def b_rows(t, jh):
+            return b_buf[jh][t % len(b_buf[jh])]
+
+        def products(t, jh):
+            c, c0 = divmod(P * t, W1_COLS)
+            for jt in range(SUB):
+                cols = slice(P * jt, P * (jt + 1))
+                for a in range(PASSES):
+                    lhs = v_w[a, jh][:, cols].bitcast(FP8X4)
+                    lhs_s = v_s[a][:, HALF * jh + P * jt : HALF * jh + P * (jt + 1)]
+                    r2 = H * a + P * t
+                    nc.tensor.matmul_mx(
+                        out=b_bank[jh][:, cols], lhsT=lhs, lhsT_scale=lhs_s,
+                        rhs=w2_w[:, 2 * r2 : 2 * (r2 + P)].bitcast(FP4X4), rhs_scale=w2_s[:, r2 : r2 + P],
+                        start=(a == 0), stop=(a == PASSES - 1),
+                    )
+                    r1 = W1_COLS * a + c0
+                    nc.tensor.matmul_mx(
+                        out=a_bank[jh][:, cols], lhsT=lhs, lhsT_scale=lhs_s,
+                        rhs=w1_w[c][:, r1 : r1 + P].bitcast(FP8X4), rhs_scale=w1_s[c][:, r1 : r1 + P],
+                        start=(a == 0), stop=(a == PASSES - 1),
+                    )
+            nc.scalar.copy(b_rows(t, jh)[:], b_bank[jh][:])
+
+        def combine(t, jh):
+            prod = h_buf[t % 2][:, HALF * jh : HALF * (jh + 1)]
+            nc.vector.scalar_tensor_tensor(prod, b_rows(t, jh)[:], 1.0, a_bank[jh][:], ADD, MULT)
+
+        def turn_h(t, jh, bank):
+            prod = h_buf[t % 2][:, HALF * jh : HALF * (jh + 1)]
+            for jt in range(SUB):
+                cols = slice(P * jt, P * (jt + 1))
+                nc.tensor.matmul(bank[:, cols], prod[:, cols], ident[:], start=True, stop=False, is_transpose=True)
+                nc.tensor.matmul(bank[:, cols], b_rows(t, jh)[:, cols], ident[:], start=False, stop=True, is_transpose=True)
+            nc.scalar.activation(prod, bank[:], ACT.Copy, scale=gain_t[:, t : t + 1])
+
+        def put_h(t):
+            if t == 0:
+                for jh in range(2):
+                    cols = slice(HALF * jh, HALF * (jh + 1))
+                    picks = list2[:, LIST_COLS * jh : LIST_COLS * (jh + 1)]
+                    nc.vector.tensor_tensor(pages[t][:].indirect(picks), h_buf[0][:, cols], wgs_t[:, cols], MULT)
+            else:
+                nc.vector.tensor_tensor(pages[t][:].indirect(list2[:]), h_buf[t % 2][:], wgs_t[:], MULT)
+
+        x_rows, x_w, x_s = {}, {}, {}
+
+        def recall(t, mh, picked):
+            picks = list3[:, LIST_COLS * mh : LIST_COLS * (mh + 1)]
+            nc.vector.tensor_copy(picked, pages[t][:].indirect(picks))
+
+        def turn_x(t, mh, picked):
+            b, tq = divmod(t, 4)
+            x_ps = x_bank[t % 2]
+            for c in range(SUB):
+                cols = slice(P * c, P * (c + 1))
+                nc.tensor.matmul(x_ps[:, cols], picked[:, cols], ident[:], start=True, stop=False, is_transpose=True)
+                nc.tensor.matmul(x_ps[:, cols], roasts[t, mh][:, cols], ident[:], start=False, stop=True, is_transpose=True)
+            if tq == 0:
+                x_rows[b, mh] = ring.tile([P, SUB * HALF], BF16, name=f"x_rows{b}_{mh}", tag="x_rows")
+            dst = x_rows[b, mh][:].rearrange("m (c u p e) -> m c u p e", c=SUB, u=2, e=2)
+            nc.scalar.copy(
+                dst[:, :, :, 32 * tq : 32 * (tq + 1), :],
+                x_ps[:].rearrange("m (c p u e) -> m c u p e", c=SUB, u=2, e=2),
+            )
+
+        def quantise_x(b, mh):
+            words = x_rows[b, mh][:].bitcast(F32)
+            grouped = ring.tile([P, 4 * HALF], BF16, name=f"xg{b}_{mh}", tag="grouped", align_bytes=64)
+            for cp in range(2):
+                w_ps = w_bank[cp]
+                for cu in range(4):
+                    src = HALF * cp + P * cu
+                    nc.tensor.transpose(w_ps[:, P * cu : P * (cu + 1)], words[:, src : src + P], ident[:])
+                nc.scalar.copy(
+                    grouped[:].bitcast(F32)[:, HALF * cp : HALF * (cp + 1)].rearrange("p (c m u) -> p c m u", c=2, u=2),
+                    w_ps[:].rearrange("p (c u m) -> p c m u", c=2, u=2),
+                )
+            x_w[b, mh] = keep.tile([P, HALF], U32, name=f"x_w{b}_{mh}", align_bytes=64)
+            x_s[b, mh] = keep.tile([P, HALF], U8, name=f"x_s{b}_{mh}", align_bytes=64)
+            nc.vector.quantize_mx(out=x_w[b, mh][:].bitcast(FP8X4), scales=x_s[b, mh][:], in_=grouped[:])
+
+        profile = {}
+
+        def write_out(mh):
+            cols = slice(HALF * mh, HALF * (mh + 1))
+            picks = list4[:, LIST_COLS * mh : LIST_COLS * (mh + 1)]
+            for nt in range(OUT_TILES):
+                y_ps = (a_bank + b_bank)[(OUT_TILES * mh + nt) % 4]
+                for b in range(PASSES):
+                    n0 = N * b + P * nt
+                    nc.tensor.matmul_mx(
+                        out=y_ps[:], lhsT=w3_w[:, n0 : n0 + P].bitcast(FP8X4), lhsT_scale=w3_s[:, n0 : n0 + P],
+                        rhs=x_w[b, mh][:].bitcast(FP8X4), rhs_scale=x_s[b, mh][:],
+                        start=(b == 0), stop=(b == PASSES - 1),
+                    )
+                y_sb = ring.tile([P, HALF], F32, name=f"y_sb{nt}_{mh}", tag="y_sb", bufs=3)
+                nc.scalar.activation(y_sb[:], y_ps[:], ACT.Abs)
+                nc.vector.tensor_tensor(profile[nt][:].indirect(picks), y_sb[:], wgo_t[:, cols], MULT)
+                if mh == 1:
+                    nc.sync.dma_start(out=out[P * nt : P * (nt + 1), :], in_=profile[nt][:])
+
+        quantise_w1(0)
+        for jh in range(2):
+            products(0, jh)
+            combine(0, jh)
+            turn_h(0, jh, w_bank[jh])
+        quantise_w1(1)
+        for jh in range(2):
+            products(1, jh)
+            combine(1, jh)
+        for t in range(ROW_TILES):
+            if t % 2 == 0 and t // 2 + 2 < H // W1_COLS:
+                quantise_w1(t // 2 + 2)
+            put_h(t)
+            for jh in range(2):
+                if t + 2 < ROW_TILES:
+                    products(t + 2, jh)
+            for jh in range(2):
+                if t + 1 < ROW_TILES:
+                    turn_h(t + 1, jh, b_bank[jh])
+            if t > 0:
+                turn_x(t - 1, 0, b_rows(t, 0)[:])
+            if t == 4:
+                quantise_x(0, 0)
+            for jh in range(2):
+                if t + 2 < ROW_TILES:
+                    combine(t + 2, jh)
+            recall(t, 0, b_rows(t + 1, 0)[:])
+        turn_x(ROW_TILES - 1, 0, b_rows(ROW_TILES, 0)[:])
+        quantise_x(1, 0)
+
+        for t in range(0, ROW_TILES, 2):
+            load_roast_second(t)
+        for nt in range(OUT_TILES):
+            if nt < 2:
+                profile[nt] = ring.tile([P, T2], F32, name=f"profile{nt}", tag="tabw")
+            else:
+                profile[nt] = keep.tile([P, T2], F32, name=f"profile{nt}", tag="tabs")
+            nc.sync.dma_start(out=profile[nt][:], in_=page1[P * nt : P * (nt + 1), :])
+
+        last_h = h_buf[(ROW_TILES - 1) % 2]
+        spare = [last_h[:, 0:HALF], last_h[:, HALF:S], wgs_t[:, 0:HALF], wgs_t[:, HALF:S]]
+        for t in range(ROW_TILES):
+            recall(t, 1, spare[t % 4])
+            turn_x(t, 1, spare[t % 4])
+            if t % 4 == 3:
+                quantise_x(t // 4, 1)
+        write_out(0)
+        write_out(1)

@@ -24,8 +24,9 @@ HALF = 512
 LIST_COLS = HALF // 16
 ROW_TILES = H // P
 OUT_TILES = N // P
-W1_COLS = 256
+W1_CHUNKS = (1, 1, 2, 2, 2)
 SUB = HALF // P
+QUARTER = HALF // 2
 
 
 def tile_list_bean_lot_recall_kernel(
@@ -37,9 +38,9 @@ def tile_list_bean_lot_recall_kernel(
         keep = ctx.enter_context(tc.tile_pool(name="keep", bufs=1))
         ring = ctx.enter_context(tc.tile_pool(name="ring", bufs=2))
         psum = ctx.enter_context(tc.psum_pool(name="psum", bufs=1))
-        a_bank = [psum.tile([P, HALF], F32, name=f"a_bank{i}") for i in range(2)]
-        b_bank = [psum.tile([P, HALF], F32, name=f"b_bank{i}") for i in range(2)]
-        x_bank = [psum.tile([P, HALF], F32, name=f"x_bank{i}") for i in range(2)]
+        a_bank = [psum.tile([P, HALF], F32, name=f"a_bank{i}") for i in range(4)]
+        b_bank = psum.tile([P, HALF], F32, name="b_bank")
+        x_bank = psum.tile([P, HALF], F32, name="x_bank")
         w_bank = [psum.tile([P, HALF], F32, name=f"w_bank{i}") for i in range(2)]
 
         def load_list(src, name):
@@ -47,25 +48,32 @@ def tile_list_bean_lot_recall_kernel(
             nc.sync.dma_start(tile[:], src)
             return tile
 
-        def load_scales(src, tile, queue):
-            nc.vector.memset(tile[:].bitcast(I32), 0)
+        def load_scales(src, tile, clearers, queue):
+            words = tile[:].bitcast(I32)
+            share = words.shape[1] // len(clearers)
+            for i, clearer in enumerate(clearers):
+                clearer.memset(words[:, share * i : share * (i + 1)], 0)
             for q in range(4):
                 queue.dma_start(
                     out=tile[32 * q : 32 * q + 4, :].bitcast(I32).rearrange("r (a c) -> r a c", a=PASSES),
                     in_=src[:, 4 * q : 4 * q + 4, :].bitcast(I32).rearrange("a r c -> r a c"),
                 )
 
-        def load_table_words(a):
-            tile = ring.tile([P, T], I32, name=f"tabw{a}", tag="tabw")
-            nc.sync.dma_start(out=tile[:], in_=tab_words[a].rearrange("p t i -> p (t i)").bitcast(I32))
+        def load_table_words(a, pieces):
+            tile = keep.tile([P, T], I32, name=f"tabw{a}", tag=f"tabw{a}", align_bytes=64)
+            words = tab_words[a].rearrange("p t i -> p (t i)").bitcast(I32)
+            width = T // pieces
+            for c0 in range(0, T, width):
+                nc.sync.dma_start(out=tile[:, c0 : c0 + width], in_=words[:, c0 : c0 + width])
             return tile
 
         w1_raw = {}
 
         def load_w1(c):
             for a in range(PASSES):
-                tile = ring.tile([P, 4, W1_COLS], F32, name=f"w1raw{c}_{a}", tag="stage", bufs=4)
-                rows = w1[HALF * a : HALF * (a + 1), W1_COLS * c : W1_COLS * (c + 1)]
+                c0, width = P * sum(W1_CHUNKS[:c]), P * W1_CHUNKS[c]
+                tile = ring.tile([P, 4, width], F32, name=f"w1raw{c}_{a}", tag="stage", bufs=4)
+                rows = w1[HALF * a : HALF * (a + 1), c0 : c0 + width]
                 nc.sync.dma_start(out=tile[:], in_=rows.rearrange("(p j) c -> p j c", j=4))
                 w1_raw[c, a] = tile
 
@@ -75,52 +83,44 @@ def tile_list_bean_lot_recall_kernel(
             pages[t] = keep.tile([P, T2], F32, name=f"page{t}")
             nc.sync.dma_start(out=pages[t][:], in_=page0[P * t : P * (t + 1), :])
 
-        def load_roast_first(t):
-            tile = keep.tile([P, HALF], F32, name=f"roast{t}")
-            nc.sync.dma_start(out=tile[:], in_=roast[P * t : P * (t + 1), 0:HALF])
-            roasts[t, 0] = tile[:]
-
-        def load_roast_second(t):
-            tile = ring.tile([P, 2, HALF], F32, name=f"roastb{t}", tag="stage", bufs=4)
-            rows = roast[P * t : P * (t + 2), HALF:PICKS]
-            nc.sync.dma_start(out=tile[:], in_=rows.rearrange("(u p) m -> p u m", u=2))
-            roasts[t, 1] = tile[:, 0, :]
-            roasts[t + 1, 1] = tile[:, 1, :]
+        def load_roast(t):
+            roasts[t] = keep.tile([P, PICKS], F32, name=f"roast{t}")
+            nc.sync.dma_start(out=roasts[t][:], in_=roast[P * t : P * (t + 1), :])
 
         list1 = load_list(offs, "list1")
         list2 = load_list(offs2, "list2")
         list3 = load_list(offs3, "list3")
         list4 = load_list(offs4, "list4")
-        tab_s = keep.tile([P, PASSES * T], U8, name="tab_s", tag="tabs")
-        load_scales(tab_scales, tab_s, nc.scalar)
-        w2_s = keep.tile([P, PASSES * H], U8, name="w2_s", align_bytes=64)
-        load_scales(w2_scales, w2_s, nc.scalar)
-        gain_rows = keep.tile([P, P], F32, name="gain_rows")
-        nc.vector.memset(gain_rows[:], 0.0)
-        nc.gpsimd.dma_start(out=gain_rows[0:ROW_TILES, :], in_=gain.rearrange("(t p) -> t p", p=P))
-        ident = keep.tile([P, P], F32, name="ident")
-        make_identity(nc, ident[:])
-        w3_s = keep.tile([P, PASSES * N], U8, name="w3_s", align_bytes=64)
-        load_scales(w3_scales, w3_s, nc.gpsimd)
-
-        tab_w = [load_table_words(0)]
+        tab_w = [load_table_words(0, 4)]
+        tab_s = keep.tile([P, PASSES * T], U8, name="tab_s", tag="tabs", align_bytes=64)
+        load_scales(tab_scales, tab_s, [nc.vector, nc.gpsimd], nc.sync)
         load_w1(0)
+        tab_w.append(load_table_words(1, 1))
+        w2_s = keep.tile([P, PASSES * H], U8, name="w2_s", align_bytes=64)
+        load_scales(w2_scales, w2_s, [nc.gpsimd], nc.sync)
         w2_w = keep.tile([P, PASSES * 2 * H], U8, name="w2_w", align_bytes=64)
         nc.sync.dma_start(
             out=w2_w[:].bitcast(I32).rearrange("p (a c) -> p a c", a=PASSES),
             in_=w2_words.bitcast(I32).rearrange("a p c -> p a c"),
         )
-        tab_w.append(load_table_words(1))
+        gain_rows = keep.tile([P, P], F32, name="gain_rows")
+        nc.gpsimd.memset(gain_rows[:], 0.0)
+        nc.sync.dma_start(out=gain_rows[0:ROW_TILES, :], in_=gain.rearrange("(t p) -> t p", p=P))
+        ident = keep.tile([P, P], F32, name="ident")
+        make_identity(nc, ident[:])
         load_w1(1)
         wgs_t = keep.tile([P, S], F32, name="wgs_t")
         nc.sync.dma_start(out=wgs_t[:], in_=wgs)
         load_page(0)
+        load_w1(2)
         for t in range(ROW_TILES):
             if t + 1 < ROW_TILES:
                 load_page(t + 1)
-            if t + 2 < H // W1_COLS:
-                load_w1(t + 2)
-            load_roast_first(t)
+            load_roast(t)
+            if t + 3 < len(W1_CHUNKS):
+                load_w1(t + 3)
+        w3_s = keep.tile([P, PASSES * N], U8, name="w3_s", align_bytes=64)
+        load_scales(w3_scales, w3_s, [nc.gpsimd], nc.sync)
         w3_w = keep.tile([P, PASSES * N], U32, name="w3_w", align_bytes=64)
         nc.sync.dma_start(
             out=w3_w[:].bitcast(I32).rearrange("p (a c) -> p a c", a=PASSES),
@@ -129,84 +129,90 @@ def tile_list_bean_lot_recall_kernel(
         wgo_t = keep.tile([P, PICKS], F32, name="wgo_t")
         nc.sync.dma_start(out=wgo_t[:], in_=wgo)
 
-        v_s, v_w = [], {}
+        v_s, v_w = [], []
         for a in range(PASSES):
             tile = keep.tile([P, S], U8, name=f"v_s{a}", align_bytes=64)
             nc.vector.tensor_copy(tile[:], tab_s[:, T * a : T * (a + 1)].indirect(list1[:]))
             v_s.append(tile)
         for a in range(PASSES):
+            tile = keep.tile([P, S], U32, name=f"v_w{a}", tag=("v_w", "tabs")[a], align_bytes=64)
             for jh in range(2):
-                tile = keep.tile([P, HALF], U32, name=f"v_w{a}_{jh}", align_bytes=64)
                 picks = list1[:, LIST_COLS * jh : LIST_COLS * (jh + 1)]
-                nc.vector.tensor_copy(tile[:], tab_w[a][:].bitcast(U32).indirect(picks))
-                v_w[a, jh] = tile
+                nc.vector.tensor_copy(tile[:, HALF * jh : HALF * (jh + 1)], tab_w[a][:].bitcast(U32).indirect(picks))
+            v_w.append(tile)
 
-        gain_ps = x_bank[0]
-        nc.tensor.transpose(gain_ps[:, 0:P], gain_rows[:], ident[:])
         gain_t = keep.tile([P, ROW_TILES], F32, name="gain_t")
-        nc.scalar.copy(gain_t[:], gain_ps[:, 0:ROW_TILES])
+
+        def turn_gain(bank):
+            nc.tensor.transpose(bank[:, 0:P], gain_rows[:], ident[:])
+            nc.scalar.copy(gain_t[:], bank[:, 0:ROW_TILES])
 
         w1_w, w1_s = {}, {}
+        staging = keep.tile([P, S], F32, name="staging", align_bytes=64)
 
         def quantise_w1(c):
-            grouped = ring.tile([P, PASSES * W1_COLS * 4], BF16, name=f"w1g{c}", tag="grouped", align_bytes=64)
+            width = P * W1_CHUNKS[c]
+            if c < 2:
+                grouped = ring.tile([P, PASSES * width * 4], BF16, name=f"w1g{c}", tag="grouped", align_bytes=64)[:]
+            else:
+                grouped = staging[:].bitcast(BF16)
             for a in range(PASSES):
-                dst = grouped[:, 4 * W1_COLS * a : 4 * W1_COLS * (a + 1)]
+                dst = grouped[:, 4 * width * a : 4 * width * (a + 1)]
                 nc.scalar.copy(
                     dst.rearrange("p (c i j) -> p c j i", i=4, j=4),
                     w1_raw[c, a][:].rearrange("p j (c i) -> p c j i", i=4),
                 )
-            w1_w[c] = keep.tile([P, PASSES * W1_COLS], U32, name=f"w1w{c}", align_bytes=64)
-            w1_s[c] = keep.tile([P, PASSES * W1_COLS], U8, name=f"w1s{c}", align_bytes=64)
-            nc.vector.quantize_mx(out=w1_w[c][:].bitcast(FP8X4), scales=w1_s[c][:], in_=grouped[:])
-
-        h_buf = [keep.tile([P, S], F32, name=f"h_buf{i}") for i in range(2)]
-        b_buf = [[keep.tile([P, HALF], F32, name=f"b_buf{jh}_{i}") for i in range(3 - jh)] for jh in range(2)]
-
-        def b_rows(t, jh):
-            return b_buf[jh][t % len(b_buf[jh])]
-
-        def products(t, jh):
-            c, c0 = divmod(P * t, W1_COLS)
-            for jt in range(SUB):
-                cols = slice(P * jt, P * (jt + 1))
+            words = keep.tile([P, PASSES * width], U32, name=f"w1w{c}", tag="tabw1" if c == 1 else f"codes{c}", align_bytes=64)
+            scales = keep.tile([P, PASSES * width], U8, name=f"w1s{c}", align_bytes=64)
+            nc.vector.quantize_mx(out=words[:].bitcast(FP8X4), scales=scales[:], in_=grouped)
+            for i in range(W1_CHUNKS[c]):
                 for a in range(PASSES):
-                    lhs = v_w[a, jh][:, cols].bitcast(FP8X4)
-                    lhs_s = v_s[a][:, HALF * jh + P * jt : HALF * jh + P * (jt + 1)]
-                    r2 = H * a + P * t
-                    nc.tensor.matmul_mx(
-                        out=b_bank[jh][:, cols], lhsT=lhs, lhsT_scale=lhs_s,
-                        rhs=w2_w[:, 2 * r2 : 2 * (r2 + P)].bitcast(FP4X4), rhs_scale=w2_s[:, r2 : r2 + P],
-                        start=(a == 0), stop=(a == PASSES - 1),
-                    )
-                    r1 = W1_COLS * a + c0
-                    nc.tensor.matmul_mx(
-                        out=a_bank[jh][:, cols], lhsT=lhs, lhsT_scale=lhs_s,
-                        rhs=w1_w[c][:, r1 : r1 + P].bitcast(FP8X4), rhs_scale=w1_s[c][:, r1 : r1 + P],
-                        start=(a == 0), stop=(a == PASSES - 1),
-                    )
-            nc.scalar.copy(b_rows(t, jh)[:], b_bank[jh][:])
+                    cols = slice(width * a + P * i, width * a + P * (i + 1))
+                    w1_w[sum(W1_CHUNKS[:c]) + i, a] = words[:, cols]
+                    w1_s[sum(W1_CHUNKS[:c]) + i, a] = scales[:, cols]
 
-        def combine(t, jh):
-            prod = h_buf[t % 2][:, HALF * jh : HALF * (jh + 1)]
-            nc.vector.scalar_tensor_tensor(prod, b_rows(t, jh)[:], 1.0, a_bank[jh][:], ADD, MULT)
+        h_buf = keep.tile([P, S], F32, name="h_buf")
+        b_buf = [keep.tile([P, S], F32, name=f"b_buf{i}") for i in range(2)]
+        pick_buf = [keep.tile([P, HALF], F32, name=f"pick_buf{i}") for i in range(2)]
 
-        def turn_h(t, jh, bank):
-            prod = h_buf[t % 2][:, HALF * jh : HALF * (jh + 1)]
-            for jt in range(SUB):
+        def h_rows(t, j0, width):
+            start = HALF if (t, j0) == (0, 0) else j0
+            return h_buf[:, start : start + width]
+
+        def b_rows(t):
+            return staging if t == 0 else b_buf[t % 2]
+
+        def products(t, j0, width, a_ps):
+            def product(bank, weights):
+                for jt in range(width // P):
+                    cols = slice(j0 + P * jt, j0 + P * (jt + 1))
+                    for a in range(PASSES):
+                        words, scales = weights(a)
+                        nc.tensor.matmul_mx(
+                            out=bank[:, P * jt : P * (jt + 1)],
+                            lhsT=v_w[a][:, cols].bitcast(FP8X4), lhsT_scale=v_s[a][:, cols],
+                            rhs=words, rhs_scale=scales, start=(a == 0), stop=(a == PASSES - 1),
+                        )
+
+            product(b_bank, lambda a: (
+                w2_w[:, 2 * (H * a + P * t) : 2 * (H * a + P * (t + 1))].bitcast(FP4X4),
+                w2_s[:, H * a + P * t : H * a + P * (t + 1)],
+            ))
+            nc.scalar.copy(b_rows(t)[:, j0 : j0 + width], b_bank[:, 0:width])
+            product(a_ps, lambda a: (w1_w[t, a].bitcast(FP8X4), w1_s[t, a]))
+
+        def combine(t, j0, width, a_ps, h_ps):
+            h_sb, b_sb = h_rows(t, j0, width), b_rows(t)[:, j0 : j0 + width]
+            nc.vector.scalar_tensor_tensor(h_sb, b_sb, 1.0, a_ps[:, 0:width], ADD, MULT)
+            for jt in range(width // P):
                 cols = slice(P * jt, P * (jt + 1))
-                nc.tensor.matmul(bank[:, cols], prod[:, cols], ident[:], start=True, stop=False, is_transpose=True)
-                nc.tensor.matmul(bank[:, cols], b_rows(t, jh)[:, cols], ident[:], start=False, stop=True, is_transpose=True)
-            nc.scalar.activation(prod, bank[:], ACT.Copy, scale=gain_t[:, t : t + 1])
+                nc.tensor.matmul(h_ps[:, cols], h_sb[:, cols], ident[:], start=True, stop=False, is_transpose=True)
+                nc.tensor.matmul(h_ps[:, cols], b_sb[:, cols], ident[:], start=False, stop=True, is_transpose=True)
+            nc.scalar.activation(h_sb, h_ps[:, 0:width], ACT.Copy, scale=gain_t[:, t : t + 1])
 
-        def put_h(t):
-            if t == 0:
-                for jh in range(2):
-                    cols = slice(HALF * jh, HALF * (jh + 1))
-                    picks = list2[:, LIST_COLS * jh : LIST_COLS * (jh + 1)]
-                    nc.vector.tensor_tensor(pages[t][:].indirect(picks), h_buf[0][:, cols], wgs_t[:, cols], MULT)
-            else:
-                nc.vector.tensor_tensor(pages[t][:].indirect(list2[:]), h_buf[t % 2][:], wgs_t[:], MULT)
+        def put_h(t, j0, width):
+            picks = list2[:, j0 // 16 : (j0 + width) // 16]
+            nc.vector.tensor_tensor(pages[t][:].indirect(picks), h_rows(t, j0, width), wgs_t[:, j0 : j0 + width], MULT)
 
         x_rows, x_w, x_s = {}, {}, {}
 
@@ -216,13 +222,13 @@ def tile_list_bean_lot_recall_kernel(
 
         def turn_x(t, mh, picked):
             b, tq = divmod(t, 4)
-            x_ps = x_bank[t % 2]
+            x_ps = b_bank if (mh == 1 and t in (4, 6)) else x_bank
             for c in range(SUB):
                 cols = slice(P * c, P * (c + 1))
                 nc.tensor.matmul(x_ps[:, cols], picked[:, cols], ident[:], start=True, stop=False, is_transpose=True)
-                nc.tensor.matmul(x_ps[:, cols], roasts[t, mh][:, cols], ident[:], start=False, stop=True, is_transpose=True)
+                nc.tensor.matmul(x_ps[:, cols], roasts[t][:, HALF * mh + P * c : HALF * mh + P * (c + 1)], ident[:], start=False, stop=True, is_transpose=True)
             if tq == 0:
-                x_rows[b, mh] = ring.tile([P, SUB * HALF], BF16, name=f"x_rows{b}_{mh}", tag="x_rows")
+                x_rows[b, mh] = ring.tile([P, SUB * HALF], BF16, name=f"x_rows{b}_{mh}", tag="x_rows", bufs=3)
             dst = x_rows[b, mh][:].rearrange("m (c u p e) -> m c u p e", c=SUB, u=2, e=2)
             nc.scalar.copy(
                 dst[:, :, :, 32 * tq : 32 * (tq + 1), :],
@@ -241,75 +247,81 @@ def tile_list_bean_lot_recall_kernel(
                     grouped[:].bitcast(F32)[:, HALF * cp : HALF * (cp + 1)].rearrange("p (c m u) -> p c m u", c=2, u=2),
                     w_ps[:].rearrange("p (c u m) -> p c m u", c=2, u=2),
                 )
-            x_w[b, mh] = keep.tile([P, HALF], U32, name=f"x_w{b}_{mh}", align_bytes=64)
+            tag = f"codes{2 + mh}" if b == 1 else f"x_w{mh}"
+            x_w[b, mh] = keep.tile([P, HALF], U32, name=f"x_w{b}_{mh}", tag=tag, align_bytes=64)
             x_s[b, mh] = keep.tile([P, HALF], U8, name=f"x_s{b}_{mh}", align_bytes=64)
             nc.vector.quantize_mx(out=x_w[b, mh][:].bitcast(FP8X4), scales=x_s[b, mh][:], in_=grouped[:])
 
         profile = {}
 
-        def write_out(mh):
-            cols = slice(HALF * mh, HALF * (mh + 1))
+        def multiply_x(mh, nt, y_ps):
+            for b in range(PASSES):
+                n0 = N * b + P * nt
+                nc.tensor.matmul_mx(
+                    out=y_ps[:], lhsT=w3_w[:, n0 : n0 + P].bitcast(FP8X4), lhsT_scale=w3_s[:, n0 : n0 + P],
+                    rhs=x_w[b, mh][:].bitcast(FP8X4), rhs_scale=x_s[b, mh][:],
+                    start=(b == 0), stop=(b == PASSES - 1),
+                )
+
+        def put_y(mh, nt, y_ps, y_sb):
             picks = list4[:, LIST_COLS * mh : LIST_COLS * (mh + 1)]
-            for nt in range(OUT_TILES):
-                y_ps = (a_bank + b_bank)[(OUT_TILES * mh + nt) % 4]
-                for b in range(PASSES):
-                    n0 = N * b + P * nt
-                    nc.tensor.matmul_mx(
-                        out=y_ps[:], lhsT=w3_w[:, n0 : n0 + P].bitcast(FP8X4), lhsT_scale=w3_s[:, n0 : n0 + P],
-                        rhs=x_w[b, mh][:].bitcast(FP8X4), rhs_scale=x_s[b, mh][:],
-                        start=(b == 0), stop=(b == PASSES - 1),
-                    )
-                y_sb = ring.tile([P, HALF], F32, name=f"y_sb{nt}_{mh}", tag="y_sb", bufs=3)
-                nc.scalar.activation(y_sb[:], y_ps[:], ACT.Abs)
-                nc.vector.tensor_tensor(profile[nt][:].indirect(picks), y_sb[:], wgo_t[:, cols], MULT)
-                if mh == 1:
-                    nc.sync.dma_start(out=out[P * nt : P * (nt + 1), :], in_=profile[nt][:])
+            nc.scalar.activation(y_sb, y_ps[:], ACT.Abs)
+            nc.vector.tensor_tensor(profile[nt][:].indirect(picks), y_sb, wgo_t[:, HALF * mh : HALF * (mh + 1)], MULT)
+
+        def a_of(t, jh):
+            return a_bank[2 * (t % 2) + jh]
 
         quantise_w1(0)
-        for jh in range(2):
-            products(0, jh)
-            combine(0, jh)
-            turn_h(0, jh, w_bank[jh])
+        products(0, 0, QUARTER, a_bank[0])
+        turn_gain(b_bank)
+        combine(0, 0, QUARTER, a_bank[0], w_bank[0])
+        products(0, QUARTER, QUARTER, a_bank[2])
+        combine(0, QUARTER, QUARTER, a_bank[2], x_bank)
+        put_h(0, 0, QUARTER)
+        products(0, HALF, HALF, a_bank[1])
+        combine(0, HALF, HALF, a_bank[1], w_bank[1])
         quantise_w1(1)
         for jh in range(2):
-            products(1, jh)
-            combine(1, jh)
+            products(1, HALF * jh, HALF, a_of(1, jh))
         for t in range(ROW_TILES):
-            if t % 2 == 0 and t // 2 + 2 < H // W1_COLS:
-                quantise_w1(t // 2 + 2)
-            put_h(t)
+            if t + 2 < len(W1_CHUNKS):
+                quantise_w1(t + 2)
             for jh in range(2):
-                if t + 2 < ROW_TILES:
-                    products(t + 2, jh)
-            for jh in range(2):
+                if (t, jh) == (0, 0):
+                    put_h(0, QUARTER, QUARTER)
+                else:
+                    put_h(t, HALF * jh, HALF)
                 if t + 1 < ROW_TILES:
-                    turn_h(t + 1, jh, b_bank[jh])
-            if t > 0:
-                turn_x(t - 1, 0, b_rows(t, 0)[:])
-            if t == 4:
-                quantise_x(0, 0)
-            for jh in range(2):
+                    combine(t + 1, HALF * jh, HALF, a_of(t + 1, jh), w_bank[jh])
                 if t + 2 < ROW_TILES:
-                    combine(t + 2, jh)
-            recall(t, 0, b_rows(t + 1, 0)[:])
-        turn_x(ROW_TILES - 1, 0, b_rows(ROW_TILES, 0)[:])
+                    products(t + 2, HALF * jh, HALF, a_of(t + 2, jh))
+            recall(t, 0, pick_buf[0][:])
+            turn_x(t, 0, pick_buf[0][:])
+            if 1 <= t <= 4:
+                recall(t - 1, 1, pick_buf[1][:])
+                turn_x(t - 1, 1, pick_buf[1][:])
+            if t in (4, 5):
+                quantise_x(0, t - 4)
         quantise_x(1, 0)
+        for nt in range(2):
+            multiply_x(0, nt, a_bank[nt])
 
-        for t in range(0, ROW_TILES, 2):
-            load_roast_second(t)
         for nt in range(OUT_TILES):
-            if nt < 2:
-                profile[nt] = ring.tile([P, T2], F32, name=f"profile{nt}", tag="tabw")
-            else:
-                profile[nt] = keep.tile([P, T2], F32, name=f"profile{nt}", tag="tabs")
+            tag = ("tabw0", "tabw1", "tabs")[nt]
+            profile[nt] = keep.tile([P, T2], F32, name=f"profile{nt}", tag=tag, align_bytes=64)
             nc.sync.dma_start(out=profile[nt][:], in_=page1[P * nt : P * (nt + 1), :])
 
-        last_h = h_buf[(ROW_TILES - 1) % 2]
-        spare = [last_h[:, 0:HALF], last_h[:, HALF:S], wgs_t[:, 0:HALF], wgs_t[:, HALF:S]]
-        for t in range(ROW_TILES):
-            recall(t, 1, spare[t % 4])
-            turn_x(t, 1, spare[t % 4])
-            if t % 4 == 3:
-                quantise_x(t // 4, 1)
-        write_out(0)
-        write_out(1)
+        spare = [h_buf[:, HALF:S], wgs_t[:, HALF:S], pick_buf[0][:], h_buf[:, 0:HALF]]
+        for t in range(4, ROW_TILES):
+            recall(t, 1, spare[t - 4])
+            turn_x(t, 1, spare[t - 4])
+        for nt in range(2):
+            put_y(0, nt, a_bank[nt], spare[nt])
+        quantise_x(1, 1)
+        multiply_x(0, 2, w_bank[1])
+        put_y(0, 2, w_bank[1], spare[2])
+        for nt in range(OUT_TILES):
+            y_ps = a_bank[(2 + nt) % 4]
+            multiply_x(1, nt, y_ps)
+            put_y(1, nt, y_ps, spare[(3 + nt) % 4])
+            nc.sync.dma_start(out=out[P * nt : P * (nt + 1), :], in_=profile[nt][:])

@@ -97,7 +97,7 @@ def tile_list_bean_lot_recall_kernel(
         load_w1(0)
         tab_w.append(load_table_words(1, 1))
         w2_s = keep.tile([P, PASSES * H], U8, name="w2_s", align_bytes=64)
-        load_scales(w2_scales, w2_s, [nc.gpsimd], nc.sync)
+        load_scales(w2_scales, w2_s, [nc.gpsimd], nc.gpsimd)
         w2_w = keep.tile([P, PASSES * 2 * H], U8, name="w2_w", align_bytes=64)
         nc.sync.dma_start(
             out=w2_w[:].bitcast(I32).rearrange("p (a c) -> p a c", a=PASSES),
@@ -105,7 +105,7 @@ def tile_list_bean_lot_recall_kernel(
         )
         gain_rows = keep.tile([P, P], F32, name="gain_rows")
         nc.gpsimd.memset(gain_rows[:], 0.0)
-        nc.sync.dma_start(out=gain_rows[0:ROW_TILES, :], in_=gain.rearrange("(t p) -> t p", p=P))
+        nc.gpsimd.dma_start(out=gain_rows[0:ROW_TILES, :], in_=gain.rearrange("(t p) -> t p", p=P))
         ident = keep.tile([P, P], F32, name="ident")
         make_identity(nc, ident[:])
         load_w1(1)
@@ -148,14 +148,14 @@ def tile_list_bean_lot_recall_kernel(
             nc.scalar.copy(gain_t[:], bank[:, 0:ROW_TILES])
 
         w1_w, w1_s = {}, {}
-        staging = keep.tile([P, S], F32, name="staging", align_bytes=64)
+        b_buf = [keep.tile([P, S], F32, name=f"b_buf{i}", align_bytes=64) for i in range(3)]
 
         def quantise_w1(c):
             width = P * W1_CHUNKS[c]
             if c < 2:
                 grouped = ring.tile([P, PASSES * width * 4], BF16, name=f"w1g{c}", tag="grouped", align_bytes=64)[:]
             else:
-                grouped = staging[:].bitcast(BF16)
+                grouped = b_buf[c - 2][:].bitcast(BF16)
             for a in range(PASSES):
                 dst = grouped[:, 4 * width * a : 4 * width * (a + 1)]
                 nc.scalar.copy(
@@ -172,7 +172,6 @@ def tile_list_bean_lot_recall_kernel(
                     w1_s[sum(W1_CHUNKS[:c]) + i, a] = scales[:, cols]
 
         h_buf = keep.tile([P, S], F32, name="h_buf")
-        b_buf = [keep.tile([P, S], F32, name=f"b_buf{i}") for i in range(2)]
         pick_buf = [keep.tile([P, HALF], F32, name=f"pick_buf{i}") for i in range(2)]
 
         def h_rows(t, j0, width):
@@ -180,9 +179,9 @@ def tile_list_bean_lot_recall_kernel(
             return h_buf[:, start : start + width]
 
         def b_rows(t):
-            return staging if t == 0 else b_buf[t % 2]
+            return b_buf[t % 3]
 
-        def products(t, j0, width, a_ps):
+        def products(t, j0, width, a_ps, b_ps):
             def product(bank, weights):
                 for jt in range(width // P):
                     cols = slice(j0 + P * jt, j0 + P * (jt + 1))
@@ -194,11 +193,11 @@ def tile_list_bean_lot_recall_kernel(
                             rhs=words, rhs_scale=scales, start=(a == 0), stop=(a == PASSES - 1),
                         )
 
-            product(b_bank, lambda a: (
+            product(b_ps, lambda a: (
                 w2_w[:, 2 * (H * a + P * t) : 2 * (H * a + P * (t + 1))].bitcast(FP4X4),
                 w2_s[:, H * a + P * t : H * a + P * (t + 1)],
             ))
-            nc.scalar.copy(b_rows(t)[:, j0 : j0 + width], b_bank[:, 0:width])
+            nc.scalar.copy(b_rows(t)[:, j0 : j0 + width], b_ps[:, 0:width])
             product(a_ps, lambda a: (w1_w[t, a].bitcast(FP8X4), w1_s[t, a]))
 
         def combine(t, j0, width, a_ps, h_ps):
@@ -272,17 +271,17 @@ def tile_list_bean_lot_recall_kernel(
             return a_bank[2 * (t % 2) + jh]
 
         quantise_w1(0)
-        products(0, 0, QUARTER, a_bank[0])
-        turn_gain(b_bank)
+        products(0, 0, QUARTER, a_bank[0], a_bank[1])
+        turn_gain(a_bank[1])
         combine(0, 0, QUARTER, a_bank[0], w_bank[0])
-        products(0, QUARTER, QUARTER, a_bank[2])
+        products(0, QUARTER, QUARTER, a_bank[2], a_bank[3])
         combine(0, QUARTER, QUARTER, a_bank[2], x_bank)
         put_h(0, 0, QUARTER)
-        products(0, HALF, HALF, a_bank[1])
+        products(0, HALF, HALF, a_bank[1], b_bank)
         combine(0, HALF, HALF, a_bank[1], w_bank[1])
         quantise_w1(1)
         for jh in range(2):
-            products(1, HALF * jh, HALF, a_of(1, jh))
+            products(1, HALF * jh, HALF, a_of(1, jh), b_bank)
         for t in range(ROW_TILES):
             if t + 2 < len(W1_CHUNKS):
                 quantise_w1(t + 2)
@@ -294,7 +293,7 @@ def tile_list_bean_lot_recall_kernel(
                 if t + 1 < ROW_TILES:
                     combine(t + 1, HALF * jh, HALF, a_of(t + 1, jh), w_bank[jh])
                 if t + 2 < ROW_TILES:
-                    products(t + 2, HALF * jh, HALF, a_of(t + 2, jh))
+                    products(t + 2, HALF * jh, HALF, a_of(t + 2, jh), b_bank)
             recall(t, 0, pick_buf[0][:])
             turn_x(t, 0, pick_buf[0][:])
             if 1 <= t <= 4:

@@ -72,7 +72,7 @@ def tile_list_bean_lot_recall_kernel(
         def load_w1(c):
             for a in range(PASSES):
                 c0, width = P * sum(W1_CHUNKS[:c]), P * W1_CHUNKS[c]
-                tile = ring.tile([P, 4, width], F32, name=f"w1raw{c}_{a}", tag="stage", bufs=4)
+                tile = ring.tile([P, 4, width], F32, name=f"w1raw{c}_{a}", tag="stage", bufs=4, align_bytes=64)
                 rows = w1[HALF * a : HALF * (a + 1), c0 : c0 + width]
                 nc.sync.dma_start(out=tile[:], in_=rows.rearrange("(p j) c -> p j c", j=4))
                 w1_raw[c, a] = tile
@@ -96,6 +96,9 @@ def tile_list_bean_lot_recall_kernel(
         load_scales(tab_scales, tab_s, [nc.vector, nc.gpsimd], nc.sync)
         load_w1(0)
         tab_w.append(load_table_words(1, 1))
+        gain_rows = keep.tile([P, P], F32, name="gain_rows")
+        nc.gpsimd.memset(gain_rows[:], 0.0)
+        nc.sync.dma_start(out=gain_rows[0:ROW_TILES, :], in_=gain.rearrange("(t p) -> t p", p=P))
         w2_s = keep.tile([P, PASSES * H], U8, name="w2_s", align_bytes=64)
         load_scales(w2_scales, w2_s, [nc.gpsimd], nc.gpsimd)
         w2_w = keep.tile([P, PASSES * 2 * H], U8, name="w2_w", align_bytes=64)
@@ -103,9 +106,6 @@ def tile_list_bean_lot_recall_kernel(
             out=w2_w[:].bitcast(I32).rearrange("p (a c) -> p a c", a=PASSES),
             in_=w2_words.bitcast(I32).rearrange("a p c -> p a c"),
         )
-        gain_rows = keep.tile([P, P], F32, name="gain_rows")
-        nc.gpsimd.memset(gain_rows[:], 0.0)
-        nc.gpsimd.dma_start(out=gain_rows[0:ROW_TILES, :], in_=gain.rearrange("(t p) -> t p", p=P))
         ident = keep.tile([P, P], F32, name="ident")
         make_identity(nc, ident[:])
         load_w1(1)
@@ -121,12 +121,12 @@ def tile_list_bean_lot_recall_kernel(
                 load_w1(t + 3)
         w3_s = keep.tile([P, PASSES * N], U8, name="w3_s", align_bytes=64)
         load_scales(w3_scales, w3_s, [nc.gpsimd], nc.sync)
-        w3_w = keep.tile([P, PASSES * N], U32, name="w3_w", align_bytes=64)
+        w3_w = ring.tile([P, PASSES * N], U32, name="w3_w", tag="stage", bufs=4, align_bytes=64)
         nc.sync.dma_start(
             out=w3_w[:].bitcast(I32).rearrange("p (a c) -> p a c", a=PASSES),
             in_=w3_words.rearrange("a p c i -> a p (c i)").bitcast(I32).rearrange("a p c -> p a c"),
         )
-        wgo_t = keep.tile([P, PICKS], F32, name="wgo_t")
+        wgo_t = ring.tile([P, PICKS], F32, name="wgo_t", tag="stage", bufs=4, align_bytes=64)
         nc.sync.dma_start(out=wgo_t[:], in_=wgo)
 
         v_s, v_w = [], []
@@ -171,12 +171,13 @@ def tile_list_bean_lot_recall_kernel(
                     w1_w[sum(W1_CHUNKS[:c]) + i, a] = words[:, cols]
                     w1_s[sum(W1_CHUNKS[:c]) + i, a] = scales[:, cols]
 
-        h_buf = keep.tile([P, S], F32, name="h_buf")
+        h_buf = [keep.tile([P, S], F32, name=f"h_buf{i}") for i in range(3)]
+        b1_buf = keep.tile([P, S], F32, name="b1_buf")
         pick_buf = [keep.tile([P, HALF], F32, name=f"pick_buf{i}") for i in range(2)]
 
         def h_rows(t, j0, width):
             start = HALF if (t, j0) == (0, 0) else j0
-            return h_buf[:, start : start + width]
+            return h_buf[t % 3][:, start : start + width]
 
         def b_rows(t):
             return b_buf[t % 3]
@@ -198,20 +199,27 @@ def tile_list_bean_lot_recall_kernel(
                 w2_s[:, H * a + P * t : H * a + P * (t + 1)],
             ))
             nc.scalar.copy(b_rows(t)[:, j0 : j0 + width], b_ps[:, 0:width])
+            if t > 0:
+                nc.scalar.activation(b1_buf[:, j0 : j0 + width], b_ps[:, 0:width], ACT.Copy, bias=1.0)
             product(a_ps, lambda a: (w1_w[t, a].bitcast(FP8X4), w1_s[t, a]))
 
         def combine(t, j0, width, a_ps, h_ps):
             h_sb, b_sb = h_rows(t, j0, width), b_rows(t)[:, j0 : j0 + width]
-            nc.vector.scalar_tensor_tensor(h_sb, b_sb, 1.0, a_ps[:, 0:width], ADD, MULT)
+            if t == 0:
+                nc.vector.scalar_tensor_tensor(h_sb, b_sb, 1.0, a_ps[:, 0:width], ADD, MULT)
+            else:
+                nc.scalar.copy(h_sb, a_ps[:, 0:width])
+                nc.gpsimd.tensor_tensor(h_sb, h_sb, b1_buf[:, j0 : j0 + width], MULT)
             for jt in range(width // P):
                 cols = slice(P * jt, P * (jt + 1))
                 nc.tensor.matmul(h_ps[:, cols], h_sb[:, cols], ident[:], start=True, stop=False, is_transpose=True)
                 nc.tensor.matmul(h_ps[:, cols], b_sb[:, cols], ident[:], start=False, stop=True, is_transpose=True)
             nc.scalar.activation(h_sb, h_ps[:, 0:width], ACT.Copy, scale=gain_t[:, t : t + 1])
+            nc.gpsimd.tensor_tensor(h_sb, h_sb, wgs_t[:, j0 : j0 + width], MULT)
 
         def put_h(t, j0, width):
             picks = list2[:, j0 // 16 : (j0 + width) // 16]
-            nc.vector.tensor_tensor(pages[t][:].indirect(picks), h_rows(t, j0, width), wgs_t[:, j0 : j0 + width], MULT)
+            nc.vector.tensor_copy(pages[t][:].indirect(picks), h_rows(t, j0, width))
 
         x_rows, x_w, x_s = {}, {}, {}
 
@@ -280,20 +288,22 @@ def tile_list_bean_lot_recall_kernel(
         products(0, HALF, HALF, a_bank[1], b_bank)
         combine(0, HALF, HALF, a_bank[1], w_bank[1])
         quantise_w1(1)
-        for jh in range(2):
-            products(1, HALF * jh, HALF, a_of(1, jh), b_bank)
+        put_h(0, QUARTER, QUARTER)
+        put_h(0, HALF, HALF)
+
+        def prepare(t):
+            for jh in range(2):
+                products(t, HALF * jh, HALF, a_of(t, jh), b_bank)
+                combine(t, HALF * jh, HALF, a_of(t, jh), w_bank[jh])
+
+        prepare(1)
         for t in range(ROW_TILES):
             if t + 2 < len(W1_CHUNKS):
                 quantise_w1(t + 2)
-            for jh in range(2):
-                if (t, jh) == (0, 0):
-                    put_h(0, QUARTER, QUARTER)
-                else:
-                    put_h(t, HALF * jh, HALF)
-                if t + 1 < ROW_TILES:
-                    combine(t + 1, HALF * jh, HALF, a_of(t + 1, jh), w_bank[jh])
-                if t + 2 < ROW_TILES:
-                    products(t + 2, HALF * jh, HALF, a_of(t + 2, jh), b_bank)
+            if t > 0:
+                put_h(t, 0, S)
+            if t + 2 < ROW_TILES:
+                prepare(t + 2)
             recall(t, 0, pick_buf[0][:])
             turn_x(t, 0, pick_buf[0][:])
             if 1 <= t <= 4:
@@ -310,7 +320,8 @@ def tile_list_bean_lot_recall_kernel(
             profile[nt] = keep.tile([P, T2], F32, name=f"profile{nt}", tag=tag, align_bytes=64)
             nc.sync.dma_start(out=profile[nt][:], in_=page1[P * nt : P * (nt + 1), :])
 
-        spare = [h_buf[:, HALF:S], wgs_t[:, HALF:S], pick_buf[0][:], h_buf[:, 0:HALF]]
+        last_h, free_h = h_buf[(ROW_TILES - 1) % 3], h_buf[ROW_TILES % 3]
+        spare = [last_h[:, 0:HALF], last_h[:, HALF:S], pick_buf[0][:], free_h[:, 0:HALF]]
         for t in range(4, ROW_TILES):
             recall(t, 1, spare[t - 4])
             turn_x(t, 1, spare[t - 4])

from contextlib import ExitStack

import concourse.mybir as mybir
from concourse.masks import make_identity

K, H, N, T, S, PICKS, T2 = 1024, 1024, 384, 4096, 1024, 1024, 2048
FLOPS = 2 * (2 * K * H * S + H * N * PICKS)

F32 = mybir.dt.float32
BF16 = mybir.dt.bfloat16
I32 = mybir.dt.int32
U32 = mybir.dt.uint32
U16 = mybir.dt.uint16
U8 = mybir.dt.uint8
FP8X4 = mybir.dt.float8_e4m3fn_x4
FP4X4 = mybir.dt.float4_e2m1fn_x4
ADD = mybir.AluOpType.add
MULT = mybir.AluOpType.mult
ACT = mybir.ActivationFunctionType

P = 128
PASSES = 2
HALF = 512
LIST_COLS = HALF // 16
ROW_TILES = H // P
OUT_TILES = N // P
W1_CHUNKS = (1, 1, 2, 2, 2)
SUB = HALF // P
QUARTER = HALF // 2


def tile_list_bean_lot_recall_kernel(
    tc, tab_words, tab_scales, offs, offs2, offs3, offs4, w1, w2_words, w2_scales,
    gain, wgs, page0, roast, w3_words, w3_scales, wgo, page1, out,
):
    nc = tc.nc
    with ExitStack() as ctx:
        keep = ctx.enter_context(tc.tile_pool(name="keep", bufs=1))
        ring = ctx.enter_context(tc.tile_pool(name="ring", bufs=2))
        psum = ctx.enter_context(tc.psum_pool(name="psum", bufs=1))
        a_bank = [psum.tile([P, HALF], F32, name=f"a_bank{i}") for i in range(4)]
        b_bank = psum.tile([P, HALF], F32, name="b_bank")
        x_bank = psum.tile([P, HALF], F32, name="x_bank")
        w_bank = [psum.tile([P, HALF], F32, name=f"w_bank{i}") for i in range(2)]

        def load_list(src, name):
            tile = keep.tile([P, S // 16], U16, name=name)
            nc.sync.dma_start(tile[:], src)
            return tile

        def load_scales(src, tile, clearers, queue):
            words = tile[:].bitcast(I32)
            share = words.shape[1] // len(clearers)
            for i, clearer in enumerate(clearers):
                clearer.memset(words[:, share * i : share * (i + 1)], 0)
            for q in range(4):
                queue.dma_start(
                    out=tile[32 * q : 32 * q + 4, :].bitcast(I32).rearrange("r (a c) -> r a c", a=PASSES),
                    in_=src[:, 4 * q : 4 * q + 4, :].bitcast(I32).rearrange("a r c -> r a c"),
                )

        def load_table_words(a, pieces):
            tile = keep.tile([P, T], I32, name=f"tabw{a}", tag=f"tabw{a}", align_bytes=64)
            words = tab_words[a].rearrange("p t i -> p (t i)").bitcast(I32)
            width = T // pieces
            for c0 in range(0, T, width):
                nc.sync.dma_start(out=tile[:, c0 : c0 + width], in_=words[:, c0 : c0 + width])
            return tile

        w1_raw = {}

        def load_w1(c):
            for a in range(PASSES):
                c0, width = P * sum(W1_CHUNKS[:c]), P * W1_CHUNKS[c]
                tile = ring.tile([P, 4, width], F32, name=f"w1raw{c}_{a}", tag="stage", bufs=4, align_bytes=64)
                rows = w1[HALF * a : HALF * (a + 1), c0 : c0 + width]
                nc.sync.dma_start(out=tile[:], in_=rows.rearrange("(p j) c -> p j c", j=4))
                w1_raw[c, a] = tile

        pages, roasts = {}, {}

        def load_page(t):
            pages[t] = keep.tile([P, T2], F32, name=f"page{t}")
            nc.sync.dma_start(out=pages[t][:], in_=page0[P * t : P * (t + 1), :])

        def load_roast(t):
            roasts[t] = keep.tile([P, PICKS], F32, name=f"roast{t}")
            nc.sync.dma_start(out=roasts[t][:], in_=roast[P * t : P * (t + 1), :])

        list1 = load_list(offs, "list1")
        list2 = load_list(offs2, "list2")
        list3 = load_list(offs3, "list3")
        list4 = load_list(offs4, "list4")
        tab_w = [load_table_words(0, 4)]
        tab_s = keep.tile([P, PASSES * T], U8, name="tab_s", tag="tabs", align_bytes=64)
        load_scales(tab_scales, tab_s, [nc.vector, nc.gpsimd], nc.sync)
        load_w1(0)
        tab_w.append(load_table_words(1, 1))
        gain_rows = keep.tile([P, P], F32, name="gain_rows")
        nc.gpsimd.memset(gain_rows[:], 0.0)
        nc.sync.dma_start(out=gain_rows[0:ROW_TILES, :], in_=gain.rearrange("(t p) -> t p", p=P))
        w2_s = keep.tile([P, PASSES * H], U8, name="w2_s", align_bytes=64)
        load_scales(w2_scales, w2_s, [nc.gpsimd], nc.gpsimd)
        w2_w = keep.tile([P, PASSES * 2 * H], U8, name="w2_w", align_bytes=64)
        nc.sync.dma_start(
            out=w2_w[:].bitcast(I32).rearrange("p (a c) -> p a c", a=PASSES),
            in_=w2_words.bitcast(I32).rearrange("a p c -> p a c"),
        )
        ident = keep.tile([P, P], F32, name="ident")
        make_identity(nc, ident[:])
        load_w1(1)
        wgs_t = keep.tile([P, S], F32, name="wgs_t")
        nc.sync.dma_start(out=wgs_t[:], in_=wgs)
        load_page(0)
        load_w1(2)
        for t in range(ROW_TILES):
            if t + 1 < ROW_TILES:
                load_page(t + 1)
            load_roast(t)
            if t + 3 < len(W1_CHUNKS):
                load_w1(t + 3)
        w3_s = keep.tile([P, PASSES * N], U8, name="w3_s", align_bytes=64)
        load_scales(w3_scales, w3_s, [nc.gpsimd], nc.sync)
        w3_w = ring.tile([P, PASSES * N], U32, name="w3_w", tag="stage", bufs=4, align_bytes=64)
        nc.sync.dma_start(
            out=w3_w[:].bitcast(I32).rearrange("p (a c) -> p a c", a=PASSES),
            in_=w3_words.rearrange("a p c i -> a p (c i)").bitcast(I32).rearrange("a p c -> p a c"),
        )
        wgo_t = ring.tile([P, PICKS], F32, name="wgo_t", tag="stage", bufs=4, align_bytes=64)
        nc.sync.dma_start(out=wgo_t[:], in_=wgo)

        v_s, v_w = [], []
        for a in range(PASSES):
            tile = keep.tile([P, S], U8, name=f"v_s{a}", align_bytes=64)
            nc.vector.tensor_copy(tile[:], tab_s[:, T * a : T * (a + 1)].indirect(list1[:]))
            v_s.append(tile)
        for a in range(PASSES):
            tile = keep.tile([P, S], U32, name=f"v_w{a}", tag=("v_w", "tabs")[a], align_bytes=64)
            for jh in range(2):
                picks = list1[:, LIST_COLS * jh : LIST_COLS * (jh + 1)]
                nc.vector.tensor_copy(tile[:, HALF * jh : HALF * (jh + 1)], tab_w[a][:].bitcast(U32).indirect(picks))
            v_w.append(tile)

        gain_t = keep.tile([P, ROW_TILES], F32, name="gain_t")

        def turn_gain(bank):
            nc.tensor.transpose(bank[:, 0:P], gain_rows[:], ident[:])
            nc.scalar.copy(gain_t[:], bank[:, 0:ROW_TILES])

        w1_w, w1_s = {}, {}
        b_buf = [keep.tile([P, S], F32, name=f"b_buf{i}", align_bytes=64) for i in range(3)]

        def quantise_w1(c):
            width = P * W1_CHUNKS[c]
            if c < 2:
                grouped = ring.tile([P, PASSES * width * 4], BF16, name=f"w1g{c}", tag="grouped", align_bytes=64)[:]
            else:
                grouped = b_buf[c - 2][:].bitcast(BF16)
            for a in range(PASSES):
                dst = grouped[:, 4 * width * a : 4 * width * (a + 1)]
                nc.scalar.copy(
                    dst.rearrange("p (c i j) -> p c j i", i=4, j=4),
                    w1_raw[c, a][:].rearrange("p j (c i) -> p c j i", i=4),
                )
            words = keep.tile([P, PASSES * width], U32, name=f"w1w{c}", tag="tabw1" if c == 1 else f"codes{c}", align_bytes=64)
            scales = keep.tile([P, PASSES * width], U8, name=f"w1s{c}", align_bytes=64)
            nc.vector.quantize_mx(out=words[:].bitcast(FP8X4), scales=scales[:], in_=grouped)
            for i in range(W1_CHUNKS[c]):
                for a in range(PASSES):
                    cols = slice(width * a + P * i, width * a + P * (i + 1))
                    w1_w[sum(W1_CHUNKS[:c]) + i, a] = words[:, cols]
                    w1_s[sum(W1_CHUNKS[:c]) + i, a] = scales[:, cols]

        h_buf = [keep.tile([P, S], F32, name=f"h_buf{i}") for i in range(3)]
        b1_buf = keep.tile([P, S], F32, name="b1_buf")
        pick_buf = [keep.tile([P, HALF], F32, name=f"pick_buf{i}") for i in range(2)]

        def h_rows(t, j0, width):
            start = HALF if (t, j0) == (0, 0) else j0
            return h_buf[t % 3][:, start : start + width]

        def b_rows(t):
            return b_buf[t % 3]

        def products(t, j0, width, a_ps, b_ps):
            def product(bank, weights):
                for jt in range(width // P):
                    cols = slice(j0 + P * jt, j0 + P * (jt + 1))
                    for a in range(PASSES):
                        words, scales = weights(a)
                        nc.tensor.matmul_mx(
                            out=bank[:, P * jt : P * (jt + 1)],
                            lhsT=v_w[a][:, cols].bitcast(FP8X4), lhsT_scale=v_s[a][:, cols],
                            rhs=words, rhs_scale=scales, start=(a == 0), stop=(a == PASSES - 1),
                        )

            product(b_ps, lambda a: (
                w2_w[:, 2 * (H * a + P * t) : 2 * (H * a + P * (t + 1))].bitcast(FP4X4),
                w2_s[:, H * a + P * t : H * a + P * (t + 1)],
            ))
            nc.scalar.copy(b_rows(t)[:, j0 : j0 + width], b_ps[:, 0:width])
            if t > 0:
                nc.scalar.activation(b1_buf[:, j0 : j0 + width], b_ps[:, 0:width], ACT.Copy, bias=1.0)
            product(a_ps, lambda a: (w1_w[t, a].bitcast(FP8X4), w1_s[t, a]))

        def combine(t, j0, width, a_ps, h_ps):
            h_sb, b_sb = h_rows(t, j0, width), b_rows(t)[:, j0 : j0 + width]
            if t == 0:
                nc.vector.scalar_tensor_tensor(h_sb, b_sb, 1.0, a_ps[:, 0:width], ADD, MULT)
            else:
                nc.scalar.copy(h_sb, a_ps[:, 0:width])
                nc.gpsimd.tensor_tensor(h_sb, h_sb, b1_buf[:, j0 : j0 + width], MULT)
            for jt in range(width // P):
                cols = slice(P * jt, P * (jt + 1))
                nc.tensor.matmul(h_ps[:, cols], h_sb[:, cols], ident[:], start=True, stop=False, is_transpose=True)
                nc.tensor.matmul(h_ps[:, cols], b_sb[:, cols], ident[:], start=False, stop=True, is_transpose=True)
            nc.scalar.activation(h_sb, h_ps[:, 0:width], ACT.Copy, scale=gain_t[:, t : t + 1])
            nc.gpsimd.tensor_tensor(h_sb, h_sb, wgs_t[:, j0 : j0 + width], MULT)

        def put_h(t, j0, width):
            picks = list2[:, j0 // 16 : (j0 + width) // 16]
            nc.vector.tensor_copy(pages[t][:].indirect(picks), h_rows(t, j0, width))

        x_rows, x_w, x_s = {}, {}, {}

        def recall(t, mh, picked):
            picks = list3[:, LIST_COLS * mh : LIST_COLS * (mh + 1)]
            nc.vector.tensor_copy(picked, pages[t][:].indirect(picks))

        def turn_x(t, mh, picked):
            b, tq = divmod(t, 4)
            x_ps = b_bank if (mh == 1 and t in (4, 6)) else x_bank
            for c in range(SUB):
                cols = slice(P * c, P * (c + 1))
                nc.tensor.matmul(x_ps[:, cols], picked[:, cols], ident[:], start=True, stop=False, is_transpose=True)
                nc.tensor.matmul(x_ps[:, cols], roasts[t][:, HALF * mh + P * c : HALF * mh + P * (c + 1)], ident[:], start=False, stop=True, is_transpose=True)
            if tq == 0:
                x_rows[b, mh] = ring.tile([P, SUB * HALF], BF16, name=f"x_rows{b}_{mh}", tag="x_rows", bufs=3)
            dst = x_rows[b, mh][:].rearrange("m (c u p e) -> m c u p e", c=SUB, u=2, e=2)
            nc.scalar.copy(
                dst[:, :, :, 32 * tq : 32 * (tq + 1), :],
                x_ps[:].rearrange("m (c p u e) -> m c u p e", c=SUB, u=2, e=2),
            )

        def quantise_x(b, mh):
            words = x_rows[b, mh][:].bitcast(F32)
            grouped = ring.tile([P, 4 * HALF], BF16, name=f"xg{b}_{mh}", tag="grouped", align_bytes=64)
            for cp in range(2):
                w_ps = w_bank[cp]
                for cu in range(4):
                    src = HALF * cp + P * cu
                    nc.tensor.transpose(w_ps[:, P * cu : P * (cu + 1)], words[:, src : src + P], ident[:])
                nc.scalar.copy(
                    grouped[:].bitcast(F32)[:, HALF * cp : HALF * (cp + 1)].rearrange("p (c m u) -> p c m u", c=2, u=2),
                    w_ps[:].rearrange("p (c u m) -> p c m u", c=2, u=2),
                )
            tag = f"codes{2 + mh}" if b == 1 else f"x_w{mh}"
            x_w[b, mh] = keep.tile([P, HALF], U32, name=f"x_w{b}_{mh}", tag=tag, align_bytes=64)
            x_s[b, mh] = keep.tile([P, HALF], U8, name=f"x_s{b}_{mh}", align_bytes=64)
            nc.vector.quantize_mx(out=x_w[b, mh][:].bitcast(FP8X4), scales=x_s[b, mh][:], in_=grouped[:])

        profile = {}

        def multiply_x(mh, nt, y_ps):
            for b in range(PASSES):
                n0 = N * b + P * nt
                nc.tensor.matmul_mx(
                    out=y_ps[:], lhsT=w3_w[:, n0 : n0 + P].bitcast(FP8X4), lhsT_scale=w3_s[:, n0 : n0 + P],
                    rhs=x_w[b, mh][:].bitcast(FP8X4), rhs_scale=x_s[b, mh][:],
                    start=(b == 0), stop=(b == PASSES - 1),
                )

        def put_y(mh, nt, y_ps, y_sb):
            picks = list4[:, LIST_COLS * mh : LIST_COLS * (mh + 1)]
            nc.scalar.activation(y_sb, y_ps[:], ACT.Abs)
            nc.vector.tensor_tensor(profile[nt][:].indirect(picks), y_sb, wgo_t[:, HALF * mh : HALF * (mh + 1)], MULT)

        def a_of(t, jh):
            return a_bank[2 * (t % 2) + jh]

        quantise_w1(0)
        products(0, 0, QUARTER, a_bank[0], a_bank[1])
        turn_gain(a_bank[1])
        combine(0, 0, QUARTER, a_bank[0], w_bank[0])
        products(0, QUARTER, QUARTER, a_bank[2], a_bank[3])
        combine(0, QUARTER, QUARTER, a_bank[2], x_bank)
        put_h(0, 0, QUARTER)
        products(0, HALF, HALF, a_bank[1], b_bank)
        combine(0, HALF, HALF, a_bank[1], w_bank[1])
        quantise_w1(1)
        put_h(0, QUARTER, QUARTER)
        put_h(0, HALF, HALF)

        def prepare(t):
            for jh in range(2):
                products(t, HALF * jh, HALF, a_of(t, jh), b_bank)
                combine(t, HALF * jh, HALF, a_of(t, jh), w_bank[jh])

        prepare(1)
        for t in range(ROW_TILES):
            if t + 2 < len(W1_CHUNKS):
                quantise_w1(t + 2)
            if t > 0:
                put_h(t, 0, S)
            if t + 2 < ROW_TILES:
                prepare(t + 2)
            recall(t, 0, pick_buf[0][:])
            turn_x(t, 0, pick_buf[0][:])
            if 1 <= t <= 4:
                recall(t - 1, 1, pick_buf[1][:])
                turn_x(t - 1, 1, pick_buf[1][:])
            if t in (4, 5):
                quantise_x(0, t - 4)
        quantise_x(1, 0)
        for nt in range(2):
            multiply_x(0, nt, a_bank[nt])

        for nt in range(OUT_TILES):
            tag = ("tabw0", "tabw1", "tabs")[nt]
            profile[nt] = keep.tile([P, T2], F32, name=f"profile{nt}", tag=tag, align_bytes=64)
            nc.sync.dma_start(out=profile[nt][:], in_=page1[P * nt : P * (nt + 1), :])

        last_h, free_h = h_buf[(ROW_TILES - 1) % 3], h_buf[ROW_TILES % 3]
        spare = [last_h[:, 0:HALF], last_h[:, HALF:S], pick_buf[0][:], free_h[:, 0:HALF]]
        for t in range(4, ROW_TILES):
            recall(t, 1, spare[t - 4])
            turn_x(t, 1, spare[t - 4])
        for nt in range(2):
            put_y(0, nt, a_bank[nt], spare[nt])
        quantise_x(1, 1)
        multiply_x(0, 2, w_bank[1])
        put_y(0, 2, w_bank[1], spare[2])
        for nt in range(OUT_TILES):
            y_ps = a_bank[(2 + nt) % 4]
            multiply_x(1, nt, y_ps)
            put_y(1, nt, y_ps, spare[(3 + nt) % 4])
            nc.sync.dma_start(out=out[P * nt : P * (nt + 1), :], in_=profile[nt][:])
